import numpy as np
import ml_dtypes


def mxq(x, axis, fmt="e4m3"):
    dtype, down = {"e4m3": (ml_dtypes.float8_e4m3fn, 7), "e5m2": (ml_dtypes.float8_e5m2, 14)}[fmt]
    v = np.moveaxis(np.asarray(x, np.float32).astype(ml_dtypes.bfloat16).astype(np.float64), axis, -1)
    blocks = v.reshape(v.shape[:-1] + (-1, 32))
    amax = np.abs(blocks).max(-1, keepdims=True)
    byte = np.maximum(np.where(amax > 0, np.frexp(amax)[1] - 1 + 127, 0) - down, 1)
    scale = np.exp2(byte - 127.0)
    codes = (blocks / scale).astype(np.float32).astype(dtype).astype(np.float64)
    return np.moveaxis((codes * scale).reshape(v.shape), -1, axis)


WIDE = False


def mx_kscale(k, group=512):
    if not WIDE:
        return np.ones(k)
    levels = np.array([18, -18])
    if group != 512:
        return np.exp2(np.random.permutation(np.resize(levels, k // group))).repeat(group)
    if k % 512:
        return np.exp2(np.random.permutation(np.resize(levels, k // 32))).repeat(32)
    a = np.empty((k // 512, 16))
    for p in range(k // 512):
        a[p, :8] = np.random.permutation(np.resize(levels, 8))
        for g in range(8):
            far = levels[np.abs(levels - a[p, g]) >= 10]
            a[p, g + 8] = far[np.random.randint(len(far))]
    return np.exp2(a.ravel()).repeat(32)


def f64(x):
    return np.asarray(x).astype(np.float64)


def silu(v):
    return v / (1.0 + np.exp(-v))


G, D, K, M, N = 4, 128, 512, 128, 512


def setup_inputs():
    n = np.random.standard_normal
    s = mx_kscale(D, 0)[:, None]
    u = mx_kscale(K)[:, None]
    return {
        "x": (n((G, D, N)) * s).astype(np.float32),
        "w1": (n((G, D, K)) / np.sqrt(D) / s).astype(np.float32),
        "hs": (np.random.uniform(0.5, 2.0, (G, K, 1)) * u).astype(np.float32),
        "w2": (n((G, K, M)) / np.sqrt(K) / u).astype(np.float32),
        "b": (0.5 * n((G, K, 1))).astype(np.float32),
        "r": n((G, M, N)).astype(np.float32),
    }


def reference(x, w1, hs, w2, b, r):
    xq = mxq(f64(x), 1, "e4m3")
    h = mxq(f64(w1), 1, "e4m3").transpose(0, 2, 1) @ xq
    h = h + f64(b)
    h = (silu(h)) * f64(hs)
    y = mxq(f64(w2), 1, "e4m3").transpose(0, 2, 1) @ mxq(h, 1, "e4m3")
    y = y + f64(r)
    return y

@@ -1,0 +1,180 @@
+from contextlib import ExitStack
+
+import concourse.mybir as mybir
+
+F32 = mybir.dt.float32
+BF16 = mybir.dt.bfloat16
+U32 = mybir.dt.uint32
+U8 = mybir.dt.uint8
+FP8X4 = mybir.dt.float8_e4m3fn_x4
+ACT = mybir.ActivationFunctionType
+ALU = mybir.AluOpType
+
+G, D, K, M, N = 4, 128, 512, 128, 512
+P = 128
+PACK = 4
+ROWS = D // PACK
+RUN = 4
+FLOPS = 2 * G * N * K * (D + M)
+
+
+def tile_rows_gmlp_silu_bias_res_kernel(tc, x, w1, hs, w2, b, r, out):
+    nc = tc.nc
+    with ExitStack() as ctx:
+        sb = ctx.enter_context(tc.tile_pool(name="sb", bufs=1))
+        ps = ctx.enter_context(tc.psum_pool(name="ps", bufs=1))
+        ctx.enter_context(tc.manual_schedule())
+
+        def sbuf(name, shape, dtype):
+            return sb.tile(shape, dtype, name=name, align_bytes=64)
+
+        def quantize(codes, scales, values):
+            nc.vector.quantize_mx(out=codes.bitcast(FP8X4), scales=scales, in_=values)
+
+        x_raw = sbuf("x_raw", [P, PACK, N], F32)
+        w1_raw = sbuf("w1_raw", [P, PACK, K], F32)
+        w2_raw = sbuf("w2_raw", [P, G, PACK * M], F32)
+        r_sb = sbuf("r_sb", [P, G, N], F32)
+        b_sb = sbuf("b_sb", [P, G, 8], F32)
+        hs_sb = sbuf("hs_sb", [P, G, 8], F32)
+
+        nc.sync.dma_start(out=x_raw[:], in_=x.rearrange("g (p t) n -> (g p) t n", t=PACK))
+        nc.sync.dma_start(out=w1_raw[:], in_=w1.rearrange("g (p t) k -> (g p) t k", t=PACK))
+        nc.sync.dma_start(out=b_sb[:, :, 0:PACK], in_=b.rearrange("g (p j) o -> p g (j o)", j=PACK))
+        nc.sync.dma_start(out=w2_raw[:], in_=w2.rearrange("g (p j) m -> p g (j m)", j=PACK))
+        nc.sync.dma_start(out=hs_sb[:, :, 0:PACK], in_=hs.rearrange("g (p j) o -> p g (j o)", j=PACK))
+        nc.sync.dma_start(out=r_sb[:], in_=r.rearrange("g m n -> m g n"))
+
+        x_bf = sbuf("x_bf", [P, N * PACK], BF16)
+        x_codes = sbuf("x_codes", [P, N], U32)
+        x_scales = sbuf("x_scales", [P, N], U8)
+        half = N // 2
+        for h in range(2):
+            nc.vector.tensor_copy(
+                out=x_bf[:, h * half * PACK : (h + 1) * half * PACK].rearrange("p (c i t) -> p c t i", i=RUN, t=PACK),
+                in_=x_raw[:, :, h * half : (h + 1) * half].rearrange("p t (c i) -> p c t i", i=RUN),
+            )
+        for h in range(2):
+            quantize(x_codes[:, h * half : (h + 1) * half], x_scales[:, h * half : (h + 1) * half],
+                     x_bf[:, h * half * PACK : (h + 1) * half * PACK])
+
+        w1_bf = [sbuf("w1_bf%d" % u, [P, 2 * P * PACK], BF16) for u in range(2)]
+        w1_codes = [sbuf("w1_codes%d" % u, [P, 2 * P], U32) for u in range(2)]
+        w1_scales = [sbuf("w1_scales%d" % u, [P, 2 * P], U8) for u in range(2)]
+        w2_bf = sbuf("w2_bf", [P, G * M * PACK], BF16)
+        w2_codes = sbuf("w2_codes", [P, G * M], U32)
+        w2_scales = sbuf("w2_scales", [P, G * M], U8)
+
+        def cast_w1(u, copy):
+            copy(
+                out=w1_bf[u][:].rearrange("p (j s t) -> p s t j", j=2, t=PACK),
+                in_=w1_raw[:].rearrange("p t (s j) -> p s t j", j=PACK)[:, :, :, 2 * u : 2 * u + 2],
+            )
+
+        cast_w1(0, nc.vector.tensor_copy)
+        cast_w1(1, nc.scalar.copy)
+        quantize(w1_codes[0][:], w1_scales[0][:], w1_bf[0][:])
+        quantize(w1_codes[1][:], w1_scales[1][:], w1_bf[1][:])
+        nc.vector.tensor_copy(
+            out=w2_bf[:].rearrange("p (g c i j) -> p g c j i", g=G, i=RUN, j=PACK),
+            in_=w2_raw[:].rearrange("p g (j c i) -> p g c j i", j=PACK, i=RUN),
+        )
+        quantize(w2_codes[:], w2_scales[:], w2_bf[:])
+
+        banks_of = [2, 2, 1, 1]
+        z_ps = [[ps.tile([P, N], F32, name="z%d_%d" % (g, i)) for i in range(banks_of[g])] for g in range(G)]
+        y_ps = [ps.tile([P, N], F32, name="y%d" % i) for i in range(2)]
+        act = [sbuf("act%d" % g, [P, PACK, N], F32) for g in range(G)]
+        h_planes = sbuf("h_planes", [P, PACK, N], BF16)
+        h_bf = [sbuf("h_bf%d" % g, [P, N * PACK], BF16) for g in range(G)]
+        h_codes = [sbuf("h_codes%d" % g, [P, N], U32) for g in range(G)]
+        h_scales = [sbuf("h_scales%d" % g, [P, N], U8) for g in range(G)]
+        y_sb = [sbuf("y_sb%d" % g, [P, N], F32) for g in range(G)]
+
+        def layer1(g, j):
+            rows = slice(g * ROWS, (g + 1) * ROWS)
+            cols = slice((j % 2) * P, (j % 2 + 1) * P)
+            bank = z_ps[g][j % banks_of[g]]
+            nc.tensor.matmul_mx(
+                out=bank[:],
+                lhsT=w1_codes[j // 2][rows, cols].bitcast(FP8X4),
+                lhsT_scale=w1_scales[j // 2][rows, cols],
+                rhs=x_codes[rows, :].bitcast(FP8X4),
+                rhs_scale=x_scales[rows, :],
+                start=True,
+                stop=True,
+            )
+            nc.scalar.activation(out=act[g][:, j, :], in_=bank[:], func=ACT.Silu, bias=b_sb[:, g, j : j + 1])
+
+        def scale_plane(g, j):
+            nc.scalar.activation(out=h_planes[:, j, :], in_=act[g][:, j, :], func=ACT.Copy, scale=hs_sb[:, g, j : j + 1])
+
+        def words(g, cols):
+            return h_bf[g][:, cols.start * PACK : cols.stop * PACK]
+
+        def scale_interleave(g):
+            nc.vector.tensor_tensor(
+                out=h_bf[g][:].rearrange("p (c i j) -> p c j i", i=RUN, j=PACK),
+                in0=act[g][:].rearrange("p j (c i) -> p c j i", i=RUN),
+                in1=hs_sb[:, g, 0:PACK].unsqueeze(1).unsqueeze(3).to_broadcast([P, N // RUN, PACK, RUN]),
+                op=ALU.mult,
+            )
+
+        def interleave(g, cols):
+            nc.vector.tensor_copy(
+                out=words(g, cols).rearrange("p (c i j) -> p c j i", i=RUN, j=PACK),
+                in_=h_planes[:, :, cols].rearrange("p j (c i) -> p c j i", i=RUN),
+            )
+
+        def quantize_h(g, cols):
+            quantize(h_codes[g][:, cols], h_scales[g][:, cols], words(g, cols))
+
+        def layer2(g):
+            cols = slice(g * M, (g + 1) * M)
+            nc.tensor.matmul_mx(
+                out=y_ps[g % 2][:],
+                lhsT=w2_codes[:, cols].bitcast(FP8X4),
+                lhsT_scale=w2_scales[:, cols],
+                rhs=h_codes[g][:].bitcast(FP8X4),
+                rhs_scale=h_scales[g][:],
+                start=True,
+                stop=True,
+            )
+
+        def finish(g):
+            nc.vector.tensor_tensor(out=y_sb[g][:], in0=y_ps[g % 2][:], in1=r_sb[:, g, :], op=ALU.add)
+            nc.sync.dma_start(out=out[g], in_=y_sb[g][:])
+
+        whole = slice(0, N)
+        halves = [slice(0, half), slice(half, N)]
+        for g, j in [(0, 0), (0, 1), (1, 0), (0, 2), (0, 3), (1, 1), (2, 0), (1, 2), (1, 3)]:
+            layer1(g, j)
+        scale_interleave(0)
+        quantize_h(0, whole)
+        layer1(2, 1)
+        layer1(3, 0)
+        scale_plane(3, 0)
+        layer1(2, 2)
+        layer1(3, 1)
+        layer2(0)
+        scale_plane(3, 1)
+        layer1(2, 3)
+        layer1(3, 2)
+        scale_plane(3, 2)
+        layer1(3, 3)
+        scale_plane(3, 3)
+        scale_interleave(1)
+        finish(0)
+        quantize_h(1, whole)
+        layer2(1)
+        scale_interleave(2)
+        finish(1)
+        quantize_h(2, whole)
+        layer2(2)
+        for cols in halves:
+            interleave(3, cols)
+        for cols in halves:
+            quantize_h(3, cols)
+        layer2(3)
+        finish(2)
+        finish(3)

@@ -15,6 +15,8 @@ P = 128
 PACK = 4
 ROWS = D // PACK
 RUN = 4
+HALF = N // 2
+NMM = 128
 FLOPS = 2 * G * N * K * (D + M)
 
 
@@ -31,150 +33,188 @@ def tile_rows_gmlp_silu_bias_res_kernel(tc, x, w1, hs, w2, b, r, out):
         def quantize(codes, scales, values):
             nc.vector.quantize_mx(out=codes.bitcast(FP8X4), scales=scales, in_=values)
 
-        x_raw = sbuf("x_raw", [P, PACK, N], F32)
+        x_raw = [sbuf("x_raw%d" % h, [P, PACK, HALF], F32) for h in range(2)]
         w1_raw = sbuf("w1_raw", [P, PACK, K], F32)
-        w2_raw = sbuf("w2_raw", [P, G, PACK * M], F32)
+        w2_raw = [sbuf("w2_raw%d" % v, [P, 2, PACK * M], F32) for v in range(2)]
         r_sb = sbuf("r_sb", [P, G, N], F32)
         b_sb = sbuf("b_sb", [P, G, 8], F32)
         hs_sb = sbuf("hs_sb", [P, G, 8], F32)
 
-        nc.sync.dma_start(out=x_raw[:], in_=x.rearrange("g (p t) n -> (g p) t n", t=PACK))
+        x_rows = x.rearrange("g (p t) n -> (g p) t n", t=PACK)
+        w2_rows = w2.rearrange("g (p j) m -> p g (j m)", j=PACK)
         nc.sync.dma_start(out=w1_raw[:], in_=w1.rearrange("g (p t) k -> (g p) t k", t=PACK))
+        nc.sync.dma_start(out=x_raw[0][:], in_=x_rows[:, :, 0:HALF])
         nc.sync.dma_start(out=b_sb[:, :, 0:PACK], in_=b.rearrange("g (p j) o -> p g (j o)", j=PACK))
-        nc.sync.dma_start(out=w2_raw[:], in_=w2.rearrange("g (p j) m -> p g (j m)", j=PACK))
+        nc.sync.dma_start(out=x_raw[1][:], in_=x_rows[:, :, HALF:N])
+        nc.sync.dma_start(out=w2_raw[0][:], in_=w2_rows[:, 0:2, :])
         nc.sync.dma_start(out=hs_sb[:, :, 0:PACK], in_=hs.rearrange("g (p j) o -> p g (j o)", j=PACK))
+        nc.sync.dma_start(out=w2_raw[1][:], in_=w2_rows[:, 2:4, :])
         nc.sync.dma_start(out=r_sb[:], in_=r.rearrange("g m n -> m g n"))
 
-        x_bf = sbuf("x_bf", [P, N * PACK], BF16)
-        x_codes = sbuf("x_codes", [P, N], U32)
-        x_scales = sbuf("x_scales", [P, N], U8)
-        half = N // 2
-        for h in range(2):
-            nc.vector.tensor_copy(
-                out=x_bf[:, h * half * PACK : (h + 1) * half * PACK].rearrange("p (c i t) -> p c t i", i=RUN, t=PACK),
-                in_=x_raw[:, :, h * half : (h + 1) * half].rearrange("p t (c i) -> p c t i", i=RUN),
-            )
-        for h in range(2):
-            quantize(x_codes[:, h * half : (h + 1) * half], x_scales[:, h * half : (h + 1) * half],
-                     x_bf[:, h * half * PACK : (h + 1) * half * PACK])
+        x_bf = [sbuf("x_bf%d" % h, [P, HALF * PACK], BF16) for h in range(2)]
+        x_codes = [sbuf("x_codes%d" % h, [P, HALF], U32) for h in range(2)]
+        x_scales = [sbuf("x_scales%d" % h, [P, HALF], U8) for h in range(2)]
+        w1_bf = [sbuf("w1_bf%d" % v, [P, 2 * P * PACK], BF16) for v in range(2)]
+        w1_codes = [sbuf("w1_codes%d" % v, [P, 2 * P], U32) for v in range(2)]
+        w1_scales = [sbuf("w1_scales%d" % v, [P, 2 * P], U8) for v in range(2)]
+        w2_bf = [sbuf("w2_bf%d" % v, [P, 2 * M * PACK], BF16) for v in range(2)]
+        w2_codes = [sbuf("w2_codes%d" % v, [P, 2 * M], U32) for v in range(2)]
+        w2_scales = [sbuf("w2_scales%d" % v, [P, 2 * M], U8) for v in range(2)]
 
-        w1_bf = [sbuf("w1_bf%d" % u, [P, 2 * P * PACK], BF16) for u in range(2)]
-        w1_codes = [sbuf("w1_codes%d" % u, [P, 2 * P], U32) for u in range(2)]
-        w1_scales = [sbuf("w1_scales%d" % u, [P, 2 * P], U8) for u in range(2)]
-        w2_bf = sbuf("w2_bf", [P, G * M * PACK], BF16)
-        w2_codes = sbuf("w2_codes", [P, G * M], U32)
-        w2_scales = sbuf("w2_scales", [P, G * M], U8)
-
-        def cast_w1(u, copy):
+        def cast_x(h, c0, c1, copy):
             copy(
-                out=w1_bf[u][:].rearrange("p (j s t) -> p s t j", j=2, t=PACK),
-                in_=w1_raw[:].rearrange("p t (s j) -> p s t j", j=PACK)[:, :, :, 2 * u : 2 * u + 2],
+                out=x_bf[h][:, c0 * PACK : c1 * PACK].rearrange("p (c i t) -> p c t i", i=RUN, t=PACK),
+                in_=x_raw[h][:, :, c0:c1].rearrange("p t (c i) -> p c t i", i=RUN),
             )
 
-        cast_w1(0, nc.vector.tensor_copy)
-        cast_w1(1, nc.scalar.copy)
-        quantize(w1_codes[0][:], w1_scales[0][:], w1_bf[0][:])
-        quantize(w1_codes[1][:], w1_scales[1][:], w1_bf[1][:])
-        nc.vector.tensor_copy(
-            out=w2_bf[:].rearrange("p (g c i j) -> p g c j i", g=G, i=RUN, j=PACK),
-            in_=w2_raw[:].rearrange("p g (j c i) -> p g c j i", j=PACK, i=RUN),
-        )
-        quantize(w2_codes[:], w2_scales[:], w2_bf[:])
+        def cast_w1(v, copy):
+            copy(
+                out=w1_bf[v][:].rearrange("p (j s t) -> p s t j", j=2, t=PACK),
+                in_=w1_raw[:].rearrange("p t (s j) -> p s t j", j=PACK)[:, :, :, 2 * v : 2 * v + 2],
+            )
+
+        def cast_w2(v, copy):
+            copy(
+                out=w2_bf[v][:].rearrange("p (g c i j) -> p g c j i", g=2, i=RUN, j=PACK),
+                in_=w2_raw[v][:].rearrange("p g (j c i) -> p g c j i", j=PACK, i=RUN),
+            )
+
+        def quantize_x(h):
+            quantize(x_codes[h][:], x_scales[h][:], x_bf[h][:])
+
+        def quantize_w1(v):
+            quantize(w1_codes[v][:], w1_scales[v][:], w1_bf[v][:])
+
+        def quantize_w2(v):
+            quantize(w2_codes[v][:], w2_scales[v][:], w2_bf[v][:])
 
         banks_of = [2, 2, 1, 1]
-        z_ps = [[ps.tile([P, N], F32, name="z%d_%d" % (g, i)) for i in range(banks_of[g])] for g in range(G)]
-        y_ps = [ps.tile([P, N], F32, name="y%d" % i) for i in range(2)]
-        act = [sbuf("act%d" % g, [P, PACK, N], F32) for g in range(G)]
-        h_planes = sbuf("h_planes", [P, PACK, N], BF16)
-        h_bf = [sbuf("h_bf%d" % g, [P, N * PACK], BF16) for g in range(G)]
-        h_codes = [sbuf("h_codes%d" % g, [P, N], U32) for g in range(G)]
-        h_scales = [sbuf("h_scales%d" % g, [P, N], U8) for g in range(G)]
-        y_sb = [sbuf("y_sb%d" % g, [P, N], F32) for g in range(G)]
+        units = [(g, h) for h in range(2) for g in range(G)]
+        z_ps = [[ps.tile([P, 2, HALF], F32, name="z%d_%d" % (g, i)) for i in range(banks_of[g])] for g in range(G)]
+        y_ps = [ps.tile([P, 2, HALF], F32, name="y%d" % i) for i in range(2)]
+        act = [sbuf("act%d" % u, [P, PACK, HALF], F32) for u in range(len(units))]
+        h_planes = [sbuf("h_planes%d" % u, [P, PACK, HALF], BF16) for u in range(len(units))]
+        h_bf = [sbuf("h_bf%d" % u, [P, HALF * PACK], BF16) for u in range(len(units))]
+        h_codes = [sbuf("h_codes%d" % u, [P, HALF], U32) for u in range(len(units))]
+        h_scales = [sbuf("h_scales%d" % u, [P, HALF], U8) for u in range(len(units))]
+        y_sb = [sbuf("y_sb%d" % u, [P, HALF], F32) for u in range(len(units))]
 
-        def layer1(g, j):
+        def layer1(u, v):
+            g, h = units[u]
             rows = slice(g * ROWS, (g + 1) * ROWS)
-            cols = slice((j % 2) * P, (j % 2 + 1) * P)
-            bank = z_ps[g][j % banks_of[g]]
-            nc.tensor.matmul_mx(
-                out=bank[:],
-                lhsT=w1_codes[j // 2][rows, cols].bitcast(FP8X4),
-                lhsT_scale=w1_scales[j // 2][rows, cols],
-                rhs=x_codes[rows, :].bitcast(FP8X4),
-                rhs_scale=x_scales[rows, :],
-                start=True,
-                stop=True,
-            )
-            nc.scalar.activation(out=act[g][:, j, :], in_=bank[:], func=ACT.Silu, bias=b_sb[:, g, j : j + 1])
+            bank = z_ps[g][v % banks_of[g]]
+            for jj in range(2):
+                cols = slice(jj * P, (jj + 1) * P)
+                for c in range(HALF // NMM):
+                    n_cols = slice(c * NMM, (c + 1) * NMM)
+                    nc.tensor.matmul_mx(
+                        out=bank[:, jj, n_cols],
+                        lhsT=w1_codes[v][rows, cols].bitcast(FP8X4),
+                        lhsT_scale=w1_scales[v][rows, cols],
+                        rhs=x_codes[h][rows, n_cols].bitcast(FP8X4),
+                        rhs_scale=x_scales[h][rows, n_cols],
+                        start=True,
+                        stop=True,
+                    )
+            for jj in range(2):
+                j = 2 * v + jj
+                nc.scalar.activation(out=act[u][:, j, :], in_=bank[:, jj, :], func=ACT.Silu, bias=b_sb[:, g, j : j + 1])
 
-        def scale_plane(g, j):
-            nc.scalar.activation(out=h_planes[:, j, :], in_=act[g][:, j, :], func=ACT.Copy, scale=hs_sb[:, g, j : j + 1])
+        def scale_planes(u):
+            g = units[u][0]
+            for j in range(PACK):
+                nc.scalar.activation(out=h_planes[u][:, j, :], in_=act[u][:, j, :], func=ACT.Copy, scale=hs_sb[:, g, j : j + 1])
 
-        def words(g, cols):
-            return h_bf[g][:, cols.start * PACK : cols.stop * PACK]
-
-        def scale_interleave(g):
+        def scale_interleave(u):
+            g = units[u][0]
             nc.vector.tensor_tensor(
-                out=h_bf[g][:].rearrange("p (c i j) -> p c j i", i=RUN, j=PACK),
-                in0=act[g][:].rearrange("p j (c i) -> p c j i", i=RUN),
-                in1=hs_sb[:, g, 0:PACK].unsqueeze(1).unsqueeze(3).to_broadcast([P, N // RUN, PACK, RUN]),
+                out=h_bf[u][:].rearrange("p (c i j) -> p c j i", i=RUN, j=PACK),
+                in0=act[u][:].rearrange("p j (c i) -> p c j i", i=RUN),
+                in1=hs_sb[:, g, 0:PACK].unsqueeze(1).unsqueeze(3).to_broadcast([P, HALF // RUN, PACK, RUN]),
                 op=ALU.mult,
             )
 
-        def interleave(g, cols):
+        def interleave(u, c0=0, c1=HALF):
             nc.vector.tensor_copy(
-                out=words(g, cols).rearrange("p (c i j) -> p c j i", i=RUN, j=PACK),
-                in_=h_planes[:, :, cols].rearrange("p j (c i) -> p c j i", i=RUN),
+                out=h_bf[u][:, c0 * PACK : c1 * PACK].rearrange("p (c i j) -> p c j i", i=RUN, j=PACK),
+                in_=h_planes[u][:, :, c0:c1].rearrange("p j (c i) -> p c j i", i=RUN),
             )
 
-        def quantize_h(g, cols):
-            quantize(h_codes[g][:, cols], h_scales[g][:, cols], words(g, cols))
+        def quantize_h(u, c0=0, c1=HALF):
+            quantize(h_codes[u][:, c0:c1], h_scales[u][:, c0:c1], h_bf[u][:, c0 * PACK : c1 * PACK])
 
-        def layer2(g):
-            cols = slice(g * M, (g + 1) * M)
-            nc.tensor.matmul_mx(
-                out=y_ps[g % 2][:],
-                lhsT=w2_codes[:, cols].bitcast(FP8X4),
-                lhsT_scale=w2_scales[:, cols],
-                rhs=h_codes[g][:].bitcast(FP8X4),
-                rhs_scale=h_scales[g][:],
-                start=True,
-                stop=True,
-            )
+        def layer2(u):
+            g = units[u][0]
+            cols = slice((g % 2) * M, (g % 2 + 1) * M)
+            for c in range(HALF // NMM):
+                n_cols = slice(c * NMM, (c + 1) * NMM)
+                nc.tensor.matmul_mx(
+                    out=y_ps[u % 2][:, 0, n_cols],
+                    lhsT=w2_codes[g // 2][:, cols].bitcast(FP8X4),
+                    lhsT_scale=w2_scales[g // 2][:, cols],
+                    rhs=h_codes[u][:, n_cols].bitcast(FP8X4),
+                    rhs_scale=h_scales[u][:, n_cols],
+                    start=True,
+                    stop=True,
+                )
 
-        def finish(g):
-            nc.vector.tensor_tensor(out=y_sb[g][:], in0=y_ps[g % 2][:], in1=r_sb[:, g, :], op=ALU.add)
-            nc.sync.dma_start(out=out[g], in_=y_sb[g][:])
+        def finish(u):
+            g, h = units[u]
+            n_cols = slice(h * HALF, (h + 1) * HALF)
+            nc.vector.tensor_tensor(out=y_sb[u][:], in0=y_ps[u % 2][:, 0, :], in1=r_sb[:, g, n_cols], op=ALU.add)
+            nc.sync.dma_start(out=out[g, :, n_cols], in_=y_sb[u][:])
 
-        whole = slice(0, N)
-        halves = [slice(0, half), slice(half, N)]
-        for g, j in [(0, 0), (0, 1), (1, 0), (0, 2), (0, 3), (1, 1), (2, 0), (1, 2), (1, 3)]:
-            layer1(g, j)
+        cast_w1(0, nc.vector.tensor_copy)
+        cast_w1(1, nc.scalar.copy)
+        quantize_w1(0)
+        cast_x(0, 0, NMM, nc.vector.tensor_copy)
+        cast_x(0, NMM, HALF, nc.scalar.copy)
+        quantize_w1(1)
+        quantize_x(0)
+        cast_x(1, 0, HALF, nc.vector.tensor_copy)
+        cast_w2(0, nc.vector.tensor_copy)
+        quantize_x(1)
+        quantize_w2(0)
+        for u, v in [(0, 0), (0, 1), (1, 0), (1, 1), (2, 0), (3, 0), (4, 0), (2, 1)]:
+            layer1(u, v)
         scale_interleave(0)
-        quantize_h(0, whole)
-        layer1(2, 1)
-        layer1(3, 0)
-        scale_plane(3, 0)
-        layer1(2, 2)
+        scale_interleave(1)
+        quantize_h(0)
+        quantize_h(1)
         layer1(3, 1)
         layer2(0)
-        scale_plane(3, 1)
-        layer1(2, 3)
-        layer1(3, 2)
-        scale_plane(3, 2)
-        layer1(3, 3)
-        scale_plane(3, 3)
-        scale_interleave(1)
-        finish(0)
-        quantize_h(1, whole)
+        layer1(4, 1)
+        layer1(5, 0)
         layer2(1)
+        cast_w2(1, nc.vector.tensor_copy)
+        finish(0)
+        quantize_w2(1)
         scale_interleave(2)
         finish(1)
-        quantize_h(2, whole)
+        quantize_h(2)
+        layer1(6, 0)
+        layer1(7, 0)
+        layer1(5, 1)
         layer2(2)
-        for cols in halves:
-            interleave(3, cols)
-        for cols in halves:
-            quantize_h(3, cols)
-        layer2(3)
-        finish(2)
-        finish(3)
+        layer1(6, 1)
+        scale_planes(5)
+        layer1(7, 1)
+        scale_planes(6)
+        scale_planes(7)
+        for u in (3, 4):
+            scale_interleave(u)
+            finish(u - 1)
+            quantize_h(u)
+            layer2(u)
+        for u in (5, 6):
+            interleave(u)
+            finish(u - 1)
+            quantize_h(u)
+            layer2(u)
+        interleave(7, 0, NMM)
+        interleave(7, NMM, HALF)
+        quantize_h(7, 0, NMM)
+        quantize_h(7, NMM, HALF)
+        layer2(7)
+        finish(6)
+        finish(7)

from contextlib import ExitStack

import concourse.mybir as mybir

F32 = mybir.dt.float32
BF16 = mybir.dt.bfloat16
U32 = mybir.dt.uint32
U8 = mybir.dt.uint8
FP8X4 = mybir.dt.float8_e4m3fn_x4
ACT = mybir.ActivationFunctionType
ALU = mybir.AluOpType

G, D, K, M, N = 4, 128, 512, 128, 512
P = 128
PACK = 4
ROWS = D // PACK
RUN = 4
HALF = N // 2
NMM = 128
FLOPS = 2 * G * N * K * (D + M)


def tile_rows_gmlp_silu_bias_res_kernel(tc, x, w1, hs, w2, b, r, out):
    nc = tc.nc
    with ExitStack() as ctx:
        sb = ctx.enter_context(tc.tile_pool(name="sb", bufs=1))
        ps = ctx.enter_context(tc.psum_pool(name="ps", bufs=1))
        ctx.enter_context(tc.manual_schedule())

        def sbuf(name, shape, dtype):
            return sb.tile(shape, dtype, name=name, align_bytes=64)

        def quantize(codes, scales, values):
            nc.vector.quantize_mx(out=codes.bitcast(FP8X4), scales=scales, in_=values)

        x_raw = [sbuf("x_raw%d" % h, [P, PACK, HALF], F32) for h in range(2)]
        w1_raw = sbuf("w1_raw", [P, PACK, K], F32)
        w2_raw = [sbuf("w2_raw%d" % v, [P, 2, PACK * M], F32) for v in range(2)]
        r_sb = sbuf("r_sb", [P, G, N], F32)
        b_sb = sbuf("b_sb", [P, G, 8], F32)
        hs_sb = sbuf("hs_sb", [P, G, 8], F32)

        x_rows = x.rearrange("g (p t) n -> (g p) t n", t=PACK)
        w2_rows = w2.rearrange("g (p j) m -> p g (j m)", j=PACK)
        nc.sync.dma_start(out=w1_raw[:], in_=w1.rearrange("g (p t) k -> (g p) t k", t=PACK))
        nc.sync.dma_start(out=x_raw[0][:], in_=x_rows[:, :, 0:HALF])
        nc.sync.dma_start(out=b_sb[:, :, 0:PACK], in_=b.rearrange("g (p j) o -> p g (j o)", j=PACK))
        nc.sync.dma_start(out=x_raw[1][:], in_=x_rows[:, :, HALF:N])
        nc.sync.dma_start(out=w2_raw[0][:], in_=w2_rows[:, 0:2, :])
        nc.sync.dma_start(out=hs_sb[:, :, 0:PACK], in_=hs.rearrange("g (p j) o -> p g (j o)", j=PACK))
        nc.sync.dma_start(out=w2_raw[1][:], in_=w2_rows[:, 2:4, :])
        nc.sync.dma_start(out=r_sb[:], in_=r.rearrange("g m n -> m g n"))

        x_bf = [sbuf("x_bf%d" % h, [P, HALF * PACK], BF16) for h in range(2)]
        x_codes = [sbuf("x_codes%d" % h, [P, HALF], U32) for h in range(2)]
        x_scales = [sbuf("x_scales%d" % h, [P, HALF], U8) for h in range(2)]
        w1_bf = [sbuf("w1_bf%d" % v, [P, 2 * P * PACK], BF16) for v in range(2)]
        w1_codes = [sbuf("w1_codes%d" % v, [P, 2 * P], U32) for v in range(2)]
        w1_scales = [sbuf("w1_scales%d" % v, [P, 2 * P], U8) for v in range(2)]
        w2_bf = [sbuf("w2_bf%d" % v, [P, 2 * M * PACK], BF16) for v in range(2)]
        w2_codes = [sbuf("w2_codes%d" % v, [P, 2 * M], U32) for v in range(2)]
        w2_scales = [sbuf("w2_scales%d" % v, [P, 2 * M], U8) for v in range(2)]

        def cast_x(h, c0, c1, copy):
            copy(
                out=x_bf[h][:, c0 * PACK : c1 * PACK].rearrange("p (c i t) -> p c t i", i=RUN, t=PACK),
                in_=x_raw[h][:, :, c0:c1].rearrange("p t (c i) -> p c t i", i=RUN),
            )

        def cast_w1(v, copy):
            copy(
                out=w1_bf[v][:].rearrange("p (j s t) -> p s t j", j=2, t=PACK),
                in_=w1_raw[:].rearrange("p t (s j) -> p s t j", j=PACK)[:, :, :, 2 * v : 2 * v + 2],
            )

        def cast_w2(v, copy):
            copy(
                out=w2_bf[v][:].rearrange("p (g c i j) -> p g c j i", g=2, i=RUN, j=PACK),
                in_=w2_raw[v][:].rearrange("p g (j c i) -> p g c j i", j=PACK, i=RUN),
            )

        def quantize_x(h):
            quantize(x_codes[h][:], x_scales[h][:], x_bf[h][:])

        def quantize_w1(v):
            quantize(w1_codes[v][:], w1_scales[v][:], w1_bf[v][:])

        def quantize_w2(v):
            quantize(w2_codes[v][:], w2_scales[v][:], w2_bf[v][:])

        banks_of = [2, 2, 1, 1]
        units = [(g, h) for h in range(2) for g in range(G)]
        z_ps = [[ps.tile([P, 2, HALF], F32, name="z%d_%d" % (g, i)) for i in range(banks_of[g])] for g in range(G)]
        y_ps = [ps.tile([P, 2, HALF], F32, name="y%d" % i) for i in range(2)]
        act = [sbuf("act%d" % u, [P, PACK, HALF], F32) for u in range(len(units))]
        h_planes = [sbuf("h_planes%d" % u, [P, PACK, HALF], BF16) for u in range(len(units))]
        h_bf = [sbuf("h_bf%d" % u, [P, HALF * PACK], BF16) for u in range(len(units))]
        h_codes = [sbuf("h_codes%d" % u, [P, HALF], U32) for u in range(len(units))]
        h_scales = [sbuf("h_scales%d" % u, [P, HALF], U8) for u in range(len(units))]
        y_sb = [sbuf("y_sb%d" % u, [P, HALF], F32) for u in range(len(units))]

        def layer1(u, v):
            g, h = units[u]
            rows = slice(g * ROWS, (g + 1) * ROWS)
            bank = z_ps[g][v % banks_of[g]]
            for jj in range(2):
                cols = slice(jj * P, (jj + 1) * P)
                for c in range(HALF // NMM):
                    n_cols = slice(c * NMM, (c + 1) * NMM)
                    nc.tensor.matmul_mx(
                        out=bank[:, jj, n_cols],
                        lhsT=w1_codes[v][rows, cols].bitcast(FP8X4),
                        lhsT_scale=w1_scales[v][rows, cols],
                        rhs=x_codes[h][rows, n_cols].bitcast(FP8X4),
                        rhs_scale=x_scales[h][rows, n_cols],
                        start=True,
                        stop=True,
                    )
            for jj in range(2):
                j = 2 * v + jj
                nc.scalar.activation(out=act[u][:, j, :], in_=bank[:, jj, :], func=ACT.Silu, bias=b_sb[:, g, j : j + 1])

        def scale_planes(u):
            g = units[u][0]
            for j in range(PACK):
                nc.scalar.activation(out=h_planes[u][:, j, :], in_=act[u][:, j, :], func=ACT.Copy, scale=hs_sb[:, g, j : j + 1])

        def scale_interleave(u):
            g = units[u][0]
            nc.vector.tensor_tensor(
                out=h_bf[u][:].rearrange("p (c i j) -> p c j i", i=RUN, j=PACK),
                in0=act[u][:].rearrange("p j (c i) -> p c j i", i=RUN),
                in1=hs_sb[:, g, 0:PACK].unsqueeze(1).unsqueeze(3).to_broadcast([P, HALF // RUN, PACK, RUN]),
                op=ALU.mult,
            )

        def interleave(u, c0=0, c1=HALF):
            nc.vector.tensor_copy(
                out=h_bf[u][:, c0 * PACK : c1 * PACK].rearrange("p (c i j) -> p c j i", i=RUN, j=PACK),
                in_=h_planes[u][:, :, c0:c1].rearrange("p j (c i) -> p c j i", i=RUN),
            )

        def quantize_h(u, c0=0, c1=HALF):
            quantize(h_codes[u][:, c0:c1], h_scales[u][:, c0:c1], h_bf[u][:, c0 * PACK : c1 * PACK])

        def layer2(u):
            g = units[u][0]
            cols = slice((g % 2) * M, (g % 2 + 1) * M)
            for c in range(HALF // NMM):
                n_cols = slice(c * NMM, (c + 1) * NMM)
                nc.tensor.matmul_mx(
                    out=y_ps[u % 2][:, 0, n_cols],
                    lhsT=w2_codes[g // 2][:, cols].bitcast(FP8X4),
                    lhsT_scale=w2_scales[g // 2][:, cols],
                    rhs=h_codes[u][:, n_cols].bitcast(FP8X4),
                    rhs_scale=h_scales[u][:, n_cols],
                    start=True,
                    stop=True,
                )

        def finish(u):
            g, h = units[u]
            n_cols = slice(h * HALF, (h + 1) * HALF)
            nc.vector.tensor_tensor(out=y_sb[u][:], in0=y_ps[u % 2][:, 0, :], in1=r_sb[:, g, n_cols], op=ALU.add)
            nc.sync.dma_start(out=out[g, :, n_cols], in_=y_sb[u][:])

        cast_w1(0, nc.vector.tensor_copy)
        cast_w1(1, nc.scalar.copy)
        quantize_w1(0)
        cast_x(0, 0, NMM, nc.vector.tensor_copy)
        cast_x(0, NMM, HALF, nc.scalar.copy)
        quantize_w1(1)
        quantize_x(0)
        cast_x(1, 0, HALF, nc.vector.tensor_copy)
        cast_w2(0, nc.vector.tensor_copy)
        quantize_x(1)
        quantize_w2(0)
        for u, v in [(0, 0), (0, 1), (1, 0), (1, 1), (2, 0), (3, 0), (4, 0), (2, 1)]:
            layer1(u, v)
        scale_interleave(0)
        scale_interleave(1)
        quantize_h(0)
        quantize_h(1)
        layer1(3, 1)
        layer2(0)
        layer1(4, 1)
        layer1(5, 0)
        layer2(1)
        cast_w2(1, nc.vector.tensor_copy)
        finish(0)
        quantize_w2(1)
        scale_interleave(2)
        finish(1)
        quantize_h(2)
        layer1(6, 0)
        layer1(7, 0)
        layer1(5, 1)
        layer2(2)
        layer1(6, 1)
        scale_planes(5)
        layer1(7, 1)
        scale_planes(6)
        scale_planes(7)
        for u in (3, 4):
            scale_interleave(u)
            finish(u - 1)
            quantize_h(u)
            layer2(u)
        for u in (5, 6):
            interleave(u)
            finish(u - 1)
            quantize_h(u)
            layer2(u)
        interleave(7, 0, NMM)
        interleave(7, NMM, HALF)
        quantize_h(7, 0, NMM)
        quantize_h(7, NMM, HALF)
        layer2(7)
        finish(6)
        finish(7)
